import numpy as np
import ml_dtypes


def mxq(x, axis, fmt="e4m3"):
    dtype, down = {"e4m3": (ml_dtypes.float8_e4m3fn, 7), "e5m2": (ml_dtypes.float8_e5m2, 14)}[fmt]
    v = np.moveaxis(np.asarray(x, np.float32).astype(ml_dtypes.bfloat16).astype(np.float64), axis, -1)
    blocks = v.reshape(v.shape[:-1] + (-1, 32))
    amax = np.abs(blocks).max(-1, keepdims=True)
    byte = np.maximum(np.where(amax > 0, np.frexp(amax)[1] - 1 + 127, 0) - down, 1)
    scale = np.exp2(byte - 127.0)
    codes = (blocks / scale).astype(np.float32).astype(dtype).astype(np.float64)
    return np.moveaxis((codes * scale).reshape(v.shape), -1, axis)


WIDE = False


def mx_kscale(k):
    if not WIDE:
        return np.ones(k)
    levels = np.array([18, -18])
    if k % 512:
        return np.exp2(np.random.permutation(np.resize(levels, k // 32))).repeat(32)
    a = np.empty((k // 512, 16))
    for p in range(k // 512):
        a[p, :8] = np.random.permutation(np.resize(levels, 8))
        for g in range(8):
            far = levels[np.abs(levels - a[p, g]) >= 10]
            a[p, g + 8] = far[np.random.randint(len(far))]
    return np.exp2(a.ravel()).repeat(32)


def f64(x):
    return np.asarray(x).astype(np.float64)


def striped(idx):
    return np.tile(np.asarray(idx).reshape(-1, 16).T, (8, 1)).astype(np.uint16)


def unstriped(offs):
    return offs[:16].T.reshape(-1).astype(np.int64)


B, N, T, D, R = 1, 512, 2048, 512, 1024
LR = 0.1
RHO = 0.9
EPS = 0.001


def setup_inputs():
    n = np.random.standard_normal
    idx = np.random.permutation(T)[:B * N]
    s = mx_kscale(D)[:, None]
    z = mx_kscale(R)[:, None]
    x = n((B, D, R))
    teach = np.exp(n((B, R, N)))
    teach = teach / teach.sum(-1, keepdims=True)
    return {
        "xT": (x * s).astype(np.float32),
        "wT": (n((D, T)) * (0.50 / np.sqrt(D)) / s).astype(np.float32),
        "y": teach.astype(np.float32),
        "wt": (np.random.uniform(0.5, 1.5, (B, R, 1)) * N / np.sqrt(R) * z).astype(np.float32),
        "xm": (x.transpose(0, 2, 1) / z).astype(np.float32),
        "vT": (np.random.uniform(0.1, 0.5, (D, T))).astype(np.float32),
        "offs": striped(idx),
    }


def reference(xT, wT, y, wt, xm, vT, offs):
    idx = unstriped(offs)
    pick = lambda x: x[:, idx].reshape(x.shape[0], B, N).transpose(1, 0, 2)
    a = mxq(f64(xT), 1, "e4m3").transpose(0, 2, 1) @ mxq(pick(f64(wT)), 1, "e4m3")
    e = np.exp(a - a.max(-1, keepdims=True))
    g = f64(wt) * (e / e.sum(-1, keepdims=True) - f64(y))
    dw = mxq(f64(xm), 1, "e4m3").transpose(0, 2, 1) @ mxq(g, 1, "e5m2")
    nv = RHO * pick(f64(vT)) + (1.0 - RHO) * dw * dw
    nw = -LR * dw / (np.sqrt(nv) + EPS)
    tables = []
    for old, new in ((wT, nw), (vT, nv),):
        table = f64(old) if old is not wT else np.zeros((D, T))
        table[:, idx] = new.transpose(1, 0, 2).reshape(D, B * N)
        tables.append(table)
    return tuple(tables)

@@ -1,0 +1,170 @@
+from contextlib import ExitStack
+import math
+
+import concourse.mybir as mybir
+
+N, T, D, R = 512, 2048, 512, 1024
+LR, RHO, EPS = 0.1, 0.9, 0.001
+FLOPS = 4 * R * N * D
+
+F32 = mybir.dt.float32
+BF16 = mybir.dt.bfloat16
+U32 = mybir.dt.uint32
+U16 = mybir.dt.uint16
+U8 = mybir.dt.uint8
+E4M3 = mybir.dt.float8_e4m3fn_x4
+E5M2 = mybir.dt.float8_e5m2_x4
+ALU = mybir.AluOpType
+ACT = mybir.ActivationFunctionType
+
+P = 128
+PACK = 4
+KP = P * PACK
+PASSES = R // KP
+DT = D // P
+
+
+def quantize(nc, pool, grouped, fmt, name):
+    codes = pool.tile([P, KP], U32, align_bytes=64, name=name + "_codes")
+    scales = pool.tile([P, KP], U8, align_bytes=64, name=name + "_scales")
+    nc.vector.quantize_mx(out=codes[:].bitcast(fmt), scales=scales[:], in_=grouped[:])
+    return codes, scales
+
+
+def tile_attend_gkl_rms_kernel(tc, xT, wT, y, wt, xm, vT, offs, out_0, out_1):
+    nc = tc.nc
+    with ExitStack() as ctx:
+        held = ctx.enter_context(tc.tile_pool(name="held", bufs=1))
+        table = ctx.enter_context(tc.tile_pool(name="table", bufs=4))
+        pair = ctx.enter_context(tc.tile_pool(name="pair", bufs=2))
+        ring = ctx.enter_context(tc.tile_pool(name="ring", bufs=4))
+        psum = ctx.enter_context(tc.psum_pool(name="psum", bufs=8))
+
+        offsets = held.tile([P, N // 16], U16, name="offsets")
+        nc.sync.dma_start(offsets[:], offs)
+        row_w = held.tile([P, PASSES, PACK], F32, name="row_w")
+        nc.sync.dma_start(row_w[:], wt[0].rearrange("(g p t) o -> p g (t o)", g=PASSES, t=PACK))
+
+        x_view = xT[0].rearrange("(p j) r -> p j r", j=PACK)
+        w_view = wT.rearrange("(p j) c -> p j c", j=PACK)
+        y_view = y[0].rearrange("(g p t) s -> g p t s", g=PASSES, t=PACK)
+        m_view = xm[0].rearrange("(g p t) d -> g p t d", g=PASSES, t=PACK)
+
+        def load(pool, tag, name, shape, src):
+            dst = pool.tile(shape, F32, tag=tag, name=name)
+            nc.sync.dma_start(dst[:], src)
+            return dst
+
+        x_raw = [None] * PASSES
+        y_raw = [None] * PASSES
+        m_raw = [None] * PASSES
+        x_raw[0] = load(pair, "x", "x_raw0", [P, PACK, KP], x_view[:, :, 0:KP])
+        w_planes = [load(table, "w", "w_plane%d" % j, [P, T], w_view[:, j, :]) for j in range(PACK)]
+        y_raw[0] = load(pair, "y", "y_raw0", [P, PACK, N], y_view[0])
+        x_raw[1] = load(pair, "x", "x_raw1", [P, PACK, KP], x_view[:, :, KP : 2 * KP])
+        y_raw[1] = load(pair, "y", "y_raw1", [P, PACK, N], y_view[1])
+        for g in range(PASSES):
+            m_raw[g] = load(pair, "m", "m_raw%d" % g, [P, PACK, D], m_view[g])
+        v_src = [load(table, "v", "v_src%d" % k, [P, T], vT[k * P : (k + 1) * P, :]) for k in range(DT)]
+
+        step_win = []
+        for k in range(DT):
+            win = table.tile([P, T], F32, tag="step", name="step_win%d" % k)
+            nc.vector.memset(win[:], 0.0)
+            step_win.append(win)
+        decay = held.tile([P, N], F32, name="decay")
+        nc.vector.memset(decay[:], 1.0)
+        nc.vector.tensor_scalar(decay[:], decay[:], RHO, None, ALU.mult)
+
+        def quantize_x(g):
+            grouped = pair.tile([P, KP * PACK], BF16, tag="xg", align_bytes=64, name="x_grouped%d" % g)
+            nc.scalar.copy(
+                grouped[:].rearrange("p (t m j) -> p m j t", t=PACK, j=PACK),
+                x_raw[g][:].rearrange("p j (m t) -> p m j t", t=PACK),
+            )
+            return quantize(nc, held, grouped, E4M3, "x%d" % g)
+
+        def quantize_m(g):
+            grouped = pair.tile([P, D * PACK], BF16, tag="mg", align_bytes=64, name="m_grouped%d" % g)
+            nc.scalar.copy(
+                grouped[:].rearrange("p (c i t) -> p c t i", i=4, t=PACK),
+                m_raw[g][:].rearrange("p t (c i) -> p c t i", i=4),
+            )
+            return quantize(nc, held, grouped, E4M3, "m%d" % g)
+
+        x_q = [quantize_x(0)]
+        w_grouped = held.tile([P, N * PACK], BF16, align_bytes=64, name="w_grouped")
+        w_slots = w_grouped[:].rearrange("p (s j) -> p s j", j=PACK)
+        for j in range(PACK):
+            nc.vector.tensor_copy(w_slots[:, :, j], w_planes[j][:].indirect(offsets[:]))
+        w_codes, w_scales = quantize(nc, held, w_grouped, E4M3, "w")
+
+        v_dst = [load(table, "w", "v_dst%d" % k, [P, T], vT[k * P : (k + 1) * P, :]) for k in range(DT)]
+
+        def gradient(g):
+            x_codes, x_scales = x_q[g]
+            neg_max = pair.tile([P, PACK], F32, tag="neg_max", name="neg_max%d" % g)
+            total = pair.tile([P, PACK], F32, tag="total", name="total%d" % g)
+            inv = pair.tile([P, PACK], F32, tag="inv", name="inv%d" % g)
+            factor = pair.tile([P, PACK], F32, tag="factor", name="factor%d" % g)
+            planes = pair.tile([P, PACK, N], BF16, tag="planes", name="planes%d" % g)
+            for t in range(PACK):
+                nc.scalar.activation(y_raw[g][:, t, :], y_raw[g][:, t, :], ACT.Copy, scale=row_w[:, g, t : t + 1])
+            exps = []
+            for t in range(PACK):
+                cols = slice(t * P, (t + 1) * P)
+                scores = psum.tile([P, N], F32, tag="bank", name="scores%d_%d" % (g, t))
+                nc.tensor.matmul_mx(
+                    out=scores[:], lhsT=x_codes[:, cols].bitcast(E4M3), lhsT_scale=x_scales[:, cols],
+                    rhs=w_codes[:].bitcast(E4M3), rhs_scale=w_scales[:], start=True, stop=True,
+                )
+                nc.vector.tensor_reduce(neg_max[:, t : t + 1], scores[:], mybir.AxisListType.X, ALU.max, negate=True)
+                e = ring.tile([P, N], F32, tag="e", name="e%d_%d" % (g, t))
+                nc.scalar.activation(e[:], scores[:], ACT.Exp, bias=neg_max[:, t : t + 1], accum_out=total[:, t : t + 1])
+                exps.append(e)
+            for h in range(2):
+                two = slice(2 * h, 2 * h + 2)
+                nc.vector.reciprocal(inv[:, two], total[:, two])
+                nc.vector.tensor_tensor(factor[:, two], inv[:, two], row_w[:, g, two], ALU.mult)
+                for t in (2 * h, 2 * h + 1):
+                    nc.vector.scalar_tensor_tensor(
+                        planes[:, t, :], exps[t][:], factor[:, t : t + 1], y_raw[g][:, t, :], ALU.mult, ALU.subtract
+                    )
+            grouped = pair.tile([P, N * PACK], BF16, tag="gg", align_bytes=64, name="g_grouped%d" % g)
+            nc.vector.tensor_copy(
+                grouped[:].rearrange("p (c i t) -> p c t i", i=4, t=PACK),
+                planes[:].rearrange("p t (c i) -> p c t i", i=4),
+            )
+            return quantize(nc, held, grouped, E5M2, "g%d" % g)
+
+        g_q = [gradient(0)]
+        x_q.append(quantize_x(1))
+        g_q.append(gradient(1))
+        m_q = [quantize_m(g) for g in range(PASSES)]
+
+        squares = pair.tile([P, DT, N], F32, tag="x", name="squares")
+        descent = pair.tile([P, DT, N], F32, tag="x", name="descent")
+        grown = pair.tile([P, DT, N], F32, tag="y", name="grown")
+        root = pair.tile([P, DT, N], F32, tag="y", name="root")
+        banks = [psum.tile([P, N], F32, tag="bank", name="dw%d" % k) for k in range(DT)]
+        for g in range(PASSES):
+            for k in range(DT):
+                cols = slice(k * P, (k + 1) * P)
+                nc.tensor.matmul_mx(
+                    out=banks[k][:], lhsT=m_q[g][0][:, cols].bitcast(E4M3), lhsT_scale=m_q[g][1][:, cols],
+                    rhs=g_q[g][0][:].bitcast(E5M2), rhs_scale=g_q[g][1][:], start=(g == 0), stop=(g == PASSES - 1),
+                )
+        for k in range(DT):
+            nc.scalar.activation(squares[:, k, :], banks[k][:], ACT.Square, scale=math.sqrt((1.0 - RHO) / RHO))
+            nc.vector.tensor_tensor(grown[:, k, :], v_src[k][:].indirect(offsets[:]), squares[:, k, :], ALU.add)
+        for k in range(DT):
+            nc.scalar.activation(descent[:, k, :], banks[k][:], ACT.Copy, scale=-LR)
+        nc.scalar.activation(root[:], grown[:], ACT.Sqrt, scale=RHO)
+        nc.scalar.activation(root[:], root[:], ACT.Square, bias=EPS)
+        nc.scalar.activation(root[:], root[:], ACT.Abs_reciprocal_sqrt)
+        for k in range(DT):
+            nc.vector.tensor_tensor(v_dst[k][:].indirect(offsets[:]), grown[:, k, :], decay[:], ALU.mult)
+            nc.sync.dma_start(out_1[k * P : (k + 1) * P, :], v_dst[k][:])
+        for k in range(DT):
+            nc.vector.tensor_tensor(step_win[k][:].indirect(offsets[:]), descent[:, k, :], root[:, k, :], ALU.mult)
+            nc.sync.dma_start(out_0[k * P : (k + 1) * P, :], step_win[k][:])

@@ -2,6 +2,7 @@ from contextlib import ExitStack
 import math
 
 import concourse.mybir as mybir
+from concourse.masks import make_identity
 
 N, T, D, R = 512, 2048, 512, 1024
 LR, RHO, EPS = 0.1, 0.9, 0.001
@@ -22,6 +23,7 @@ PACK = 4
 KP = P * PACK
 PASSES = R // KP
 DT = D // P
+WINDOWS = 3
 
 
 def quantize(nc, pool, grouped, fmt, name):
@@ -37,13 +39,10 @@ def tile_attend_gkl_rms_kernel(tc, xT, wT, y, wt, xm, vT, offs, out_0, out_1):
         held = ctx.enter_context(tc.tile_pool(name="held", bufs=1))
         table = ctx.enter_context(tc.tile_pool(name="table", bufs=4))
         pair = ctx.enter_context(tc.tile_pool(name="pair", bufs=2))
-        ring = ctx.enter_context(tc.tile_pool(name="ring", bufs=4))
         psum = ctx.enter_context(tc.psum_pool(name="psum", bufs=8))
 
         offsets = held.tile([P, N // 16], U16, name="offsets")
-        nc.sync.dma_start(offsets[:], offs)
         row_w = held.tile([P, PASSES, PACK], F32, name="row_w")
-        nc.sync.dma_start(row_w[:], wt[0].rearrange("(g p t) o -> p g (t o)", g=PASSES, t=PACK))
 
         x_view = xT[0].rearrange("(p j) r -> p j r", j=PACK)
         w_view = wT.rearrange("(p j) c -> p j c", j=PACK)
@@ -58,30 +57,34 @@ def tile_attend_gkl_rms_kernel(tc, xT, wT, y, wt, xm, vT, offs, out_0, out_1):
         x_raw = [None] * PASSES
         y_raw = [None] * PASSES
         m_raw = [None] * PASSES
+        w_planes = [load(table, "w", "w_plane0", [P, T], w_view[:, 0, :])]
+        nc.sync.dma_start(offsets[:], offs)
+        w_planes.extend(load(table, "w", "w_plane%d" % j, [P, T], w_view[:, j, :]) for j in range(1, PACK))
         x_raw[0] = load(pair, "x", "x_raw0", [P, PACK, KP], x_view[:, :, 0:KP])
-        w_planes = [load(table, "w", "w_plane%d" % j, [P, T], w_view[:, j, :]) for j in range(PACK)]
-        y_raw[0] = load(pair, "y", "y_raw0", [P, PACK, N], y_view[0])
         x_raw[1] = load(pair, "x", "x_raw1", [P, PACK, KP], x_view[:, :, KP : 2 * KP])
+        nc.sync.dma_start(row_w[:], wt[0].rearrange("(g p t) o -> p g (t o)", g=PASSES, t=PACK))
+        y_raw[0] = load(pair, "y", "y_raw0", [P, PACK, N], y_view[0])
         y_raw[1] = load(pair, "y", "y_raw1", [P, PACK, N], y_view[1])
         for g in range(PASSES):
             m_raw[g] = load(pair, "m", "m_raw%d" % g, [P, PACK, D], m_view[g])
         v_src = [load(table, "v", "v_src%d" % k, [P, T], vT[k * P : (k + 1) * P, :]) for k in range(DT)]
 
         step_win = []
-        for k in range(DT):
-            win = table.tile([P, T], F32, tag="step", name="step_win%d" % k)
+        for k in range(WINDOWS):
+            win = held.tile([P, T], F32, name="step_win%d" % k)
             nc.vector.memset(win[:], 0.0)
             step_win.append(win)
-        decay = held.tile([P, N], F32, name="decay")
-        nc.vector.memset(decay[:], 1.0)
-        nc.vector.tensor_scalar(decay[:], decay[:], RHO, None, ALU.mult)
 
-        def quantize_x(g):
+        ident = held.tile([P, P], F32, name="ident")
+        make_identity(nc, ident[:])
+
+        def quantize_x(g, on_vector):
             grouped = pair.tile([P, KP * PACK], BF16, tag="xg", align_bytes=64, name="x_grouped%d" % g)
-            nc.scalar.copy(
-                grouped[:].rearrange("p (t m j) -> p m j t", t=PACK, j=PACK),
-                x_raw[g][:].rearrange("p j (m t) -> p m j t", t=PACK),
-            )
+            dst = grouped[:].rearrange("p (t m j) -> p m j t", t=PACK, j=PACK)
+            src = x_raw[g][:].rearrange("p j (m t) -> p m j t", t=PACK)
+            if on_vector:
+                nc.vector.tensor_copy(dst[:, :on_vector], src[:, :on_vector])
+            nc.scalar.copy(dst[:, on_vector:], src[:, on_vector:])
             return quantize(nc, held, grouped, E4M3, "x%d" % g)
 
         def quantize_m(g):
@@ -92,25 +95,22 @@ def tile_attend_gkl_rms_kernel(tc, xT, wT, y, wt, xm, vT, offs, out_0, out_1):
             )
             return quantize(nc, held, grouped, E4M3, "m%d" % g)
 
-        x_q = [quantize_x(0)]
         w_grouped = held.tile([P, N * PACK], BF16, align_bytes=64, name="w_grouped")
         w_slots = w_grouped[:].rearrange("p (s j) -> p s j", j=PACK)
         for j in range(PACK):
             nc.vector.tensor_copy(w_slots[:, :, j], w_planes[j][:].indirect(offsets[:]))
         w_codes, w_scales = quantize(nc, held, w_grouped, E4M3, "w")
+        x_q = [quantize_x(0, 80)]
 
         v_dst = [load(table, "w", "v_dst%d" % k, [P, T], vT[k * P : (k + 1) * P, :]) for k in range(DT)]
 
-        def gradient(g):
+        x_q.append(quantize_x(1, 0))
+
+        def softmax_parts(g):
             x_codes, x_scales = x_q[g]
             neg_max = pair.tile([P, PACK], F32, tag="neg_max", name="neg_max%d" % g)
             total = pair.tile([P, PACK], F32, tag="total", name="total%d" % g)
-            inv = pair.tile([P, PACK], F32, tag="inv", name="inv%d" % g)
-            factor = pair.tile([P, PACK], F32, tag="factor", name="factor%d" % g)
-            planes = pair.tile([P, PACK, N], BF16, tag="planes", name="planes%d" % g)
-            for t in range(PACK):
-                nc.scalar.activation(y_raw[g][:, t, :], y_raw[g][:, t, :], ACT.Copy, scale=row_w[:, g, t : t + 1])
-            exps = []
+            exps = pair.tile([P, PACK, N], F32, tag="e", name="exps%d" % g)
             for t in range(PACK):
                 cols = slice(t * P, (t + 1) * P)
                 scores = psum.tile([P, N], F32, tag="bank", name="scores%d_%d" % (g, t))
@@ -119,33 +119,46 @@ def tile_attend_gkl_rms_kernel(tc, xT, wT, y, wt, xm, vT, offs, out_0, out_1):
                     rhs=w_codes[:].bitcast(E4M3), rhs_scale=w_scales[:], start=True, stop=True,
                 )
                 nc.vector.tensor_reduce(neg_max[:, t : t + 1], scores[:], mybir.AxisListType.X, ALU.max, negate=True)
-                e = ring.tile([P, N], F32, tag="e", name="e%d_%d" % (g, t))
-                nc.scalar.activation(e[:], scores[:], ACT.Exp, bias=neg_max[:, t : t + 1], accum_out=total[:, t : t + 1])
-                exps.append(e)
-            for h in range(2):
-                two = slice(2 * h, 2 * h + 2)
-                nc.vector.reciprocal(inv[:, two], total[:, two])
-                nc.vector.tensor_tensor(factor[:, two], inv[:, two], row_w[:, g, two], ALU.mult)
-                for t in (2 * h, 2 * h + 1):
-                    nc.vector.scalar_tensor_tensor(
-                        planes[:, t, :], exps[t][:], factor[:, t : t + 1], y_raw[g][:, t, :], ALU.mult, ALU.subtract
-                    )
+                nc.scalar.activation(
+                    exps[:, t, :], scores[:], ACT.Exp, bias=neg_max[:, t : t + 1], accum_out=total[:, t : t + 1]
+                )
+            for t in range(PACK):
+                if g == 0:
+                    nc.vector.tensor_scalar(y_raw[g][:, t, :], y_raw[g][:, t, :], row_w[:, g, t : t + 1], None, ALU.mult)
+                else:
+                    nc.scalar.activation(y_raw[g][:, t, :], y_raw[g][:, t, :], ACT.Copy, scale=row_w[:, g, t : t + 1])
+            return exps, total
+
+        def gradient(g, exps, total):
+            inv = pair.tile([P, PACK], F32, tag="inv", name="inv%d" % g)
+            factor = pair.tile([P, PACK], F32, tag="factor", name="factor%d" % g)
+            planes = pair.tile([P, PACK, N], BF16, tag="planes", name="planes%d" % g)
+            nc.vector.reciprocal(inv[:], total[:])
+            nc.vector.tensor_tensor(factor[:], inv[:], row_w[:, g, :], ALU.mult)
+            for t in range(PACK):
+                nc.vector.scalar_tensor_tensor(
+                    planes[:, t, :], exps[:, t, :], factor[:, t : t + 1], y_raw[g][:, t, :], ALU.mult, ALU.subtract
+                )
             grouped = pair.tile([P, N * PACK], BF16, tag="gg", align_bytes=64, name="g_grouped%d" % g)
-            nc.vector.tensor_copy(
+            weave = nc.vector.tensor_copy if g == 0 else nc.scalar.copy
+            weave(
                 grouped[:].rearrange("p (c i t) -> p c t i", i=4, t=PACK),
                 planes[:].rearrange("p t (c i) -> p c t i", i=4),
             )
             return quantize(nc, held, grouped, E5M2, "g%d" % g)
 
-        g_q = [gradient(0)]
-        x_q.append(quantize_x(1))
-        g_q.append(gradient(1))
-        m_q = [quantize_m(g) for g in range(PASSES)]
+        parts = [softmax_parts(g) for g in range(PASSES)]
+        g_q = []
+        m_q = []
+        for g in range(PASSES):
+            m_q.append(quantize_m(g))
+            g_q.append(gradient(g, *parts[g]))
 
+        kept = held.tile([P, DT, N], F32, name="kept")
         squares = pair.tile([P, DT, N], F32, tag="x", name="squares")
         descent = pair.tile([P, DT, N], F32, tag="x", name="descent")
-        grown = pair.tile([P, DT, N], F32, tag="y", name="grown")
-        root = pair.tile([P, DT, N], F32, tag="y", name="root")
+        turned = pair.tile([P, DT, N], F32, tag="y", name="turned")
+        inverse = pair.tile([P, DT, N], F32, tag="y", name="inverse")
         banks = [psum.tile([P, N], F32, tag="bank", name="dw%d" % k) for k in range(DT)]
         for g in range(PASSES):
             for k in range(DT):
@@ -155,16 +168,26 @@ def tile_attend_gkl_rms_kernel(tc, xT, wT, y, wt, xm, vT, offs, out_0, out_1):
                     rhs=g_q[g][0][:].bitcast(E5M2), rhs_scale=g_q[g][1][:], start=(g == 0), stop=(g == PASSES - 1),
                 )
         for k in range(DT):
-            nc.scalar.activation(squares[:, k, :], banks[k][:], ACT.Square, scale=math.sqrt((1.0 - RHO) / RHO))
-            nc.vector.tensor_tensor(grown[:, k, :], v_src[k][:].indirect(offsets[:]), squares[:, k, :], ALU.add)
-        for k in range(DT):
-            nc.scalar.activation(descent[:, k, :], banks[k][:], ACT.Copy, scale=-LR)
-        nc.scalar.activation(root[:], grown[:], ACT.Sqrt, scale=RHO)
-        nc.scalar.activation(root[:], root[:], ACT.Square, bias=EPS)
-        nc.scalar.activation(root[:], root[:], ACT.Abs_reciprocal_sqrt)
-        for k in range(DT):
-            nc.vector.tensor_tensor(v_dst[k][:].indirect(offsets[:]), grown[:, k, :], decay[:], ALU.mult)
+            nc.scalar.activation(squares[:, k, :], banks[k][:], ACT.Square, scale=math.sqrt(1.0 - RHO))
+            nc.vector.tensor_scalar(kept[:, k, :], v_src[k][:].indirect(offsets[:]), RHO, 0.0, ALU.mult, ALU.add)
+            nc.vector.tensor_tensor(v_dst[k][:].indirect(offsets[:]), kept[:, k, :], squares[:, k, :], ALU.add)
             nc.sync.dma_start(out_1[k * P : (k + 1) * P, :], v_dst[k][:])
         for k in range(DT):
-            nc.vector.tensor_tensor(step_win[k][:].indirect(offsets[:]), descent[:, k, :], root[:, k, :], ALU.mult)
-            nc.sync.dma_start(out_0[k * P : (k + 1) * P, :], step_win[k][:])
+            grown = psum.tile([P, N], F32, tag="bank", name="grown%d" % k)
+            for c in range(N // P):
+                cols = slice(c * P, (c + 1) * P)
+                nc.tensor.matmul(grown[:, cols], kept[:, k, cols], ident[:], start=True, stop=False, is_transpose=True)
+                nc.tensor.matmul(grown[:, cols], squares[:, k, cols], ident[:], start=False, stop=True, is_transpose=True)
+            nc.scalar.activation(turned[:, k, :], grown[:], ACT.Sqrt)
+        nc.scalar.activation(turned[:], turned[:], ACT.Square, bias=EPS)
+        for k in range(DT):
+            nc.scalar.activation(turned[:, k, :], turned[:, k, :], ACT.Abs_reciprocal_sqrt)
+            back = psum.tile([P, N], F32, tag="bank", name="back%d" % k)
+            for c in range(N // P):
+                cols = slice(c * P, (c + 1) * P)
+                nc.tensor.transpose(back[:, cols], turned[:, k, cols], ident[:])
+            nc.scalar.activation(descent[:, k, :], banks[k][:], ACT.Copy, scale=-LR)
+            nc.scalar.copy(inverse[:, k, :], back[:])
+            win = step_win[k % WINDOWS]
+            nc.vector.tensor_tensor(win[:].indirect(offsets[:]), descent[:, k, :], inverse[:, k, :], ALU.mult)
+            nc.sync.dma_start(out_0[k * P : (k + 1) * P, :], win[:])

@@ -26,10 +26,14 @@ DT = D // P
 WINDOWS = 3
 
 
-def quantize(nc, pool, grouped, fmt, name):
+def quantize(nc, pool, grouped, fmt, name, calls=1):
     codes = pool.tile([P, KP], U32, align_bytes=64, name=name + "_codes")
     scales = pool.tile([P, KP], U8, align_bytes=64, name=name + "_scales")
-    nc.vector.quantize_mx(out=codes[:].bitcast(fmt), scales=scales[:], in_=grouped[:])
+    width = KP // calls
+    for c in range(calls):
+        words = slice(c * width, (c + 1) * width)
+        values = slice(c * width * PACK, (c + 1) * width * PACK)
+        nc.vector.quantize_mx(out=codes[:, words].bitcast(fmt), scales=scales[:, words], in_=grouped[:, values])
     return codes, scales
 
 
@@ -85,7 +89,7 @@ def tile_attend_gkl_rms_kernel(tc, xT, wT, y, wt, xm, vT, offs, out_0, out_1):
             if on_vector:
                 nc.vector.tensor_copy(dst[:, :on_vector], src[:, :on_vector])
             nc.scalar.copy(dst[:, on_vector:], src[:, on_vector:])
-            return quantize(nc, held, grouped, E4M3, "x%d" % g)
+            return quantize(nc, held, grouped, E4M3, "x%d" % g, PACK)
 
         def quantize_m(g):
             grouped = pair.tile([P, D * PACK], BF16, tag="mg", align_bytes=64, name="m_grouped%d" % g)
@@ -145,6 +149,9 @@ def tile_attend_gkl_rms_kernel(tc, xT, wT, y, wt, xm, vT, offs, out_0, out_1):
                 grouped[:].rearrange("p (c i t) -> p c t i", i=4, t=PACK),
                 planes[:].rearrange("p t (c i) -> p c t i", i=4),
             )
+            if g == PASSES - 1:
+                warm = held.tile([P, 1], F32, name="warm")
+                nc.scalar.activation(warm[:], grouped[:, 0:1], ACT.Sqrt, scale=0.0, bias=1.0)
             return quantize(nc, held, grouped, E5M2, "g%d" % g)
 
         parts = [softmax_parts(g) for g in range(PASSES)]

@@ -71,7 +71,6 @@ def tile_attend_gkl_rms_kernel(tc, xT, wT, y, wt, xm, vT, offs, out_0, out_1):
         y_raw[1] = load(pair, "y", "y_raw1", [P, PACK, N], y_view[1])
         for g in range(PASSES):
             m_raw[g] = load(pair, "m", "m_raw%d" % g, [P, PACK, D], m_view[g])
-        v_src = [load(table, "v", "v_src%d" % k, [P, T], vT[k * P : (k + 1) * P, :]) for k in range(DT)]
 
         step_win = []
         for k in range(WINDOWS):
@@ -97,6 +96,9 @@ def tile_attend_gkl_rms_kernel(tc, xT, wT, y, wt, xm, vT, offs, out_0, out_1):
                 grouped[:].rearrange("p (c i t) -> p c t i", i=4, t=PACK),
                 m_raw[g][:].rearrange("p t (c i) -> p c t i", i=4),
             )
+            if g == PASSES - 1:
+                warm = held.tile([P, 1], F32, name="warm")
+                nc.scalar.activation(warm[:], grouped[:, 0:1], ACT.Sqrt, scale=0.0, bias=1.0)
             return quantize(nc, held, grouped, E4M3, "m%d" % g)
 
         w_grouped = held.tile([P, N * PACK], BF16, align_bytes=64, name="w_grouped")
@@ -106,7 +108,13 @@ def tile_attend_gkl_rms_kernel(tc, xT, wT, y, wt, xm, vT, offs, out_0, out_1):
         w_codes, w_scales = quantize(nc, held, w_grouped, E4M3, "w")
         x_q = [quantize_x(0, 80)]
 
-        v_dst = [load(table, "w", "v_dst%d" % k, [P, T], vT[k * P : (k + 1) * P, :]) for k in range(DT)]
+        def load_v(tag, k):
+            return load(table, tag, "v_%s%d" % (tag, k), [P, T], vT[k * P : (k + 1) * P, :])
+
+        v_src = [load_v("v", k) for k in range(3)]
+        v_dst = [load_v("w", 0)]
+        v_src.extend(load_v("v", k) for k in range(3, DT))
+        v_dst.extend(load_v("w", k) for k in range(1, DT))
 
         x_q.append(quantize_x(1, 0))
 
@@ -128,7 +136,7 @@ def tile_attend_gkl_rms_kernel(tc, xT, wT, y, wt, xm, vT, offs, out_0, out_1):
                 )
             for t in range(PACK):
                 if g == 0:
-                    nc.vector.tensor_scalar(y_raw[g][:, t, :], y_raw[g][:, t, :], row_w[:, g, t : t + 1], None, ALU.mult)
+                    nc.gpsimd.tensor_scalar(y_raw[g][:, t, :], y_raw[g][:, t, :], row_w[:, g, t : t + 1], 0.0, ALU.mult, ALU.add)
                 else:
                     nc.scalar.activation(y_raw[g][:, t, :], y_raw[g][:, t, :], ACT.Copy, scale=row_w[:, g, t : t + 1])
             return exps, total
@@ -144,14 +152,10 @@ def tile_attend_gkl_rms_kernel(tc, xT, wT, y, wt, xm, vT, offs, out_0, out_1):
                     planes[:, t, :], exps[:, t, :], factor[:, t : t + 1], y_raw[g][:, t, :], ALU.mult, ALU.subtract
                 )
             grouped = pair.tile([P, N * PACK], BF16, tag="gg", align_bytes=64, name="g_grouped%d" % g)
-            weave = nc.vector.tensor_copy if g == 0 else nc.scalar.copy
-            weave(
+            nc.vector.tensor_copy(
                 grouped[:].rearrange("p (c i t) -> p c t i", i=4, t=PACK),
                 planes[:].rearrange("p t (c i) -> p c t i", i=4),
             )
-            if g == PASSES - 1:
-                warm = held.tile([P, 1], F32, name="warm")
-                nc.scalar.activation(warm[:], grouped[:, 0:1], ACT.Sqrt, scale=0.0, bias=1.0)
             return quantize(nc, held, grouped, E5M2, "g%d" % g)
 
         parts = [softmax_parts(g) for g in range(PASSES)]

@@ -22,8 +22,20 @@ P = 128
 PACK = 4
 KP = P * PACK
 PASSES = R // KP
-DT = D // P
+D_TILES = D // P
+RUN = 4
+STEPS = 128
+X_ON_VECTOR = (80, 0)
+G_ON_VECTOR = (STEPS, 48)
 WINDOWS = 3
+EARLY_V = 3
+
+
+def weave(nc, dst, src, on_vector):
+    if on_vector > 0:
+        nc.vector.tensor_copy(dst[:, :on_vector], src[:, :on_vector])
+    if on_vector < STEPS:
+        nc.scalar.copy(dst[:, on_vector:], src[:, on_vector:])
 
 
 def quantize(nc, pool, grouped, fmt, name, calls=1):
@@ -41,8 +53,8 @@ def tile_attend_gkl_rms_kernel(tc, xT, wT, y, wt, xm, vT, offs, out_0, out_1):
     nc = tc.nc
     with ExitStack() as ctx:
         held = ctx.enter_context(tc.tile_pool(name="held", bufs=1))
-        table = ctx.enter_context(tc.tile_pool(name="table", bufs=4))
-        pair = ctx.enter_context(tc.tile_pool(name="pair", bufs=2))
+        table = ctx.enter_context(tc.tile_pool(name="table", bufs=D_TILES))
+        pair = ctx.enter_context(tc.tile_pool(name="pair", bufs=PASSES))
         psum = ctx.enter_context(tc.psum_pool(name="psum", bufs=8))
 
         offsets = held.tile([P, N // 16], U16, name="offsets")
@@ -58,68 +70,64 @@ def tile_attend_gkl_rms_kernel(tc, xT, wT, y, wt, xm, vT, offs, out_0, out_1):
             nc.sync.dma_start(dst[:], src)
             return dst
 
-        x_raw = [None] * PASSES
-        y_raw = [None] * PASSES
-        m_raw = [None] * PASSES
         w_planes = [load(table, "w", "w_plane0", [P, T], w_view[:, 0, :])]
         nc.sync.dma_start(offsets[:], offs)
         w_planes.extend(load(table, "w", "w_plane%d" % j, [P, T], w_view[:, j, :]) for j in range(1, PACK))
-        x_raw[0] = load(pair, "x", "x_raw0", [P, PACK, KP], x_view[:, :, 0:KP])
-        x_raw[1] = load(pair, "x", "x_raw1", [P, PACK, KP], x_view[:, :, KP : 2 * KP])
+        x_raw = [
+            load(pair, "x", "x_raw%d" % g, [P, PACK, KP], x_view[:, :, g * KP : (g + 1) * KP]) for g in range(PASSES)
+        ]
         nc.sync.dma_start(row_w[:], wt[0].rearrange("(g p t) o -> p g (t o)", g=PASSES, t=PACK))
-        y_raw[0] = load(pair, "y", "y_raw0", [P, PACK, N], y_view[0])
-        y_raw[1] = load(pair, "y", "y_raw1", [P, PACK, N], y_view[1])
-        for g in range(PASSES):
-            m_raw[g] = load(pair, "m", "m_raw%d" % g, [P, PACK, D], m_view[g])
+        targets = [load(pair, "y", "targets%d" % g, [P, PACK, N], y_view[g]) for g in range(PASSES)]
+        m_raw = [load(pair, "m", "m_raw%d" % g, [P, PACK, D], m_view[g]) for g in range(PASSES)]
 
-        step_win = []
+        step_windows = []
         for k in range(WINDOWS):
-            win = held.tile([P, T], F32, name="step_win%d" % k)
-            nc.vector.memset(win[:], 0.0)
-            step_win.append(win)
+            window = held.tile([P, T], F32, name="step_window%d" % k)
+            nc.vector.memset(window[:], 0.0)
+            step_windows.append(window)
 
         ident = held.tile([P, P], F32, name="ident")
         make_identity(nc, ident[:])
 
-        def quantize_x(g, on_vector):
+        def quantize_x(g):
             grouped = pair.tile([P, KP * PACK], BF16, tag="xg", align_bytes=64, name="x_grouped%d" % g)
-            dst = grouped[:].rearrange("p (t m j) -> p m j t", t=PACK, j=PACK)
-            src = x_raw[g][:].rearrange("p j (m t) -> p m j t", t=PACK)
-            if on_vector:
-                nc.vector.tensor_copy(dst[:, :on_vector], src[:, :on_vector])
-            nc.scalar.copy(dst[:, on_vector:], src[:, on_vector:])
+            weave(
+                nc,
+                grouped[:].rearrange("p (t m j) -> p m j t", t=PACK, j=PACK),
+                x_raw[g][:].rearrange("p j (m t) -> p m j t", t=PACK),
+                X_ON_VECTOR[g],
+            )
             return quantize(nc, held, grouped, E4M3, "x%d" % g, PACK)
 
-        def quantize_m(g):
-            grouped = pair.tile([P, D * PACK], BF16, tag="mg", align_bytes=64, name="m_grouped%d" % g)
-            nc.scalar.copy(
-                grouped[:].rearrange("p (c i t) -> p c t i", i=4, t=PACK),
-                m_raw[g][:].rearrange("p t (c i) -> p c t i", i=4),
+        def quantize_rows(planes, tag, name, fmt, on_vector):
+            grouped = pair.tile([P, KP * PACK], BF16, tag=tag, align_bytes=64, name=name + "_grouped")
+            weave(
+                nc,
+                grouped[:].rearrange("p (c i t) -> p c t i", i=RUN, t=PACK),
+                planes[:].rearrange("p t (c i) -> p c t i", i=RUN),
+                on_vector,
             )
-            if g == PASSES - 1:
-                warm = held.tile([P, 1], F32, name="warm")
-                nc.scalar.activation(warm[:], grouped[:, 0:1], ACT.Sqrt, scale=0.0, bias=1.0)
-            return quantize(nc, held, grouped, E4M3, "m%d" % g)
+            return quantize(nc, held, grouped, fmt, name)
 
         w_grouped = held.tile([P, N * PACK], BF16, align_bytes=64, name="w_grouped")
         w_slots = w_grouped[:].rearrange("p (s j) -> p s j", j=PACK)
         for j in range(PACK):
             nc.vector.tensor_copy(w_slots[:, :, j], w_planes[j][:].indirect(offsets[:]))
         w_codes, w_scales = quantize(nc, held, w_grouped, E4M3, "w")
-        x_q = [quantize_x(0, 80)]
+        x_quantised = [quantize_x(0)]
 
         def load_v(tag, k):
             return load(table, tag, "v_%s%d" % (tag, k), [P, T], vT[k * P : (k + 1) * P, :])
 
-        v_src = [load_v("v", k) for k in range(3)]
+        v_src = [load_v("v", k) for k in range(EARLY_V)]
         v_dst = [load_v("w", 0)]
-        v_src.extend(load_v("v", k) for k in range(3, DT))
-        v_dst.extend(load_v("w", k) for k in range(1, DT))
+        v_src.extend(load_v("v", k) for k in range(EARLY_V, D_TILES))
+        v_dst.extend(load_v("w", k) for k in range(1, D_TILES))
 
-        x_q.append(quantize_x(1, 0))
+        x_quantised.append(quantize_x(1))
 
         def softmax_parts(g):
-            x_codes, x_scales = x_q[g]
+            x_codes, x_scales = x_quantised[g]
             neg_max = pair.tile([P, PACK], F32, tag="neg_max", name="neg_max%d" % g)
             total = pair.tile([P, PACK], F32, tag="total", name="total%d" % g)
             exps = pair.tile([P, PACK, N], F32, tag="e", name="exps%d" % g)
@@ -135,10 +143,11 @@ def tile_attend_gkl_rms_kernel(tc, xT, wT, y, wt, xm, vT, offs, out_0, out_1):
                     exps[:, t, :], scores[:], ACT.Exp, bias=neg_max[:, t : t + 1], accum_out=total[:, t : t + 1]
                 )
             for t in range(PACK):
+                rows = targets[g][:, t, :]
                 if g == 0:
-                    nc.gpsimd.tensor_scalar(y_raw[g][:, t, :], y_raw[g][:, t, :], row_w[:, g, t : t + 1], 0.0, ALU.mult, ALU.add)
+                    nc.gpsimd.tensor_scalar(rows, rows, row_w[:, g, t : t + 1], 0.0, ALU.mult, ALU.add)
                 else:
-                    nc.scalar.activation(y_raw[g][:, t, :], y_raw[g][:, t, :], ACT.Copy, scale=row_w[:, g, t : t + 1])
+                    nc.scalar.activation(rows, rows, ACT.Copy, scale=row_w[:, g, t : t + 1])
             return exps, total
 
         def gradient(g, exps, total):
@@ -149,56 +158,58 @@ def tile_attend_gkl_rms_kernel(tc, xT, wT, y, wt, xm, vT, offs, out_0, out_1):
             nc.vector.tensor_tensor(factor[:], inv[:], row_w[:, g, :], ALU.mult)
             for t in range(PACK):
                 nc.vector.scalar_tensor_tensor(
-                    planes[:, t, :], exps[:, t, :], factor[:, t : t + 1], y_raw[g][:, t, :], ALU.mult, ALU.subtract
+                    planes[:, t, :], exps[:, t, :], factor[:, t : t + 1], targets[g][:, t, :], ALU.mult, ALU.subtract
                 )
-            grouped = pair.tile([P, N * PACK], BF16, tag="gg", align_bytes=64, name="g_grouped%d" % g)
-            nc.vector.tensor_copy(
-                grouped[:].rearrange("p (c i t) -> p c t i", i=4, t=PACK),
-                planes[:].rearrange("p t (c i) -> p c t i", i=4),
-            )
-            return quantize(nc, held, grouped, E5M2, "g%d" % g)
+            return quantize_rows(planes, "gg", "g%d" % g, E5M2, G_ON_VECTOR[g])
 
         parts = [softmax_parts(g) for g in range(PASSES)]
-        g_q = []
-        m_q = []
+        g_quantised = []
+        m_quantised = []
         for g in range(PASSES):
-            m_q.append(quantize_m(g))
-            g_q.append(gradient(g, *parts[g]))
+            m_quantised.append(quantize_rows(m_raw[g], "mg", "m%d" % g, E4M3, 0))
+            g_quantised.append(gradient(g, *parts[g]))
 
-        kept = held.tile([P, DT, N], F32, name="kept")
-        squares = pair.tile([P, DT, N], F32, tag="x", name="squares")
-        descent = pair.tile([P, DT, N], F32, tag="x", name="descent")
-        turned = pair.tile([P, DT, N], F32, tag="y", name="turned")
-        inverse = pair.tile([P, DT, N], F32, tag="y", name="inverse")
-        banks = [psum.tile([P, N], F32, tag="bank", name="dw%d" % k) for k in range(DT)]
+        kept = held.tile([P, D_TILES, N], F32, name="kept")
+        squares = pair.tile([P, D_TILES, N], F32, tag="x", name="squares")
+        descent = pair.tile([P, D_TILES, N], F32, tag="x", name="descent")
+        turned = pair.tile([P, D_TILES, N], F32, tag="y", name="turned")
+        inverse = pair.tile([P, D_TILES, N], F32, tag="y", name="inverse")
+
+        dw = [psum.tile([P, N], F32, tag="bank", name="dw%d" % k) for k in range(D_TILES)]
         for g in range(PASSES):
-            for k in range(DT):
+            m_codes, m_scales = m_quantised[g]
+            g_codes, g_scales = g_quantised[g]
+            for k in range(D_TILES):
                 cols = slice(k * P, (k + 1) * P)
                 nc.tensor.matmul_mx(
-                    out=banks[k][:], lhsT=m_q[g][0][:, cols].bitcast(E4M3), lhsT_scale=m_q[g][1][:, cols],
-                    rhs=g_q[g][0][:].bitcast(E5M2), rhs_scale=g_q[g][1][:], start=(g == 0), stop=(g == PASSES - 1),
+                    out=dw[k][:], lhsT=m_codes[:, cols].bitcast(E4M3), lhsT_scale=m_scales[:, cols],
+                    rhs=g_codes[:].bitcast(E5M2), rhs_scale=g_scales[:], start=(g == 0), stop=(g == PASSES - 1),
                 )
-        for k in range(DT):
-            nc.scalar.activation(squares[:, k, :], banks[k][:], ACT.Square, scale=math.sqrt(1.0 - RHO))
+
+        for k in range(D_TILES):
+            nc.scalar.activation(squares[:, k, :], dw[k][:], ACT.Square, scale=math.sqrt(1.0 - RHO))
             nc.vector.tensor_scalar(kept[:, k, :], v_src[k][:].indirect(offsets[:]), RHO, 0.0, ALU.mult, ALU.add)
             nc.vector.tensor_tensor(v_dst[k][:].indirect(offsets[:]), kept[:, k, :], squares[:, k, :], ALU.add)
             nc.sync.dma_start(out_1[k * P : (k + 1) * P, :], v_dst[k][:])
-        for k in range(DT):
+
+        for k in range(D_TILES):
             grown = psum.tile([P, N], F32, tag="bank", name="grown%d" % k)
             for c in range(N // P):
                 cols = slice(c * P, (c + 1) * P)
                 nc.tensor.matmul(grown[:, cols], kept[:, k, cols], ident[:], start=True, stop=False, is_transpose=True)
                 nc.tensor.matmul(grown[:, cols], squares[:, k, cols], ident[:], start=False, stop=True, is_transpose=True)
             nc.scalar.activation(turned[:, k, :], grown[:], ACT.Sqrt)
+
         nc.scalar.activation(turned[:], turned[:], ACT.Square, bias=EPS)
-        for k in range(DT):
+
+        for k in range(D_TILES):
             nc.scalar.activation(turned[:, k, :], turned[:, k, :], ACT.Abs_reciprocal_sqrt)
             back = psum.tile([P, N], F32, tag="bank", name="back%d" % k)
             for c in range(N // P):
                 cols = slice(c * P, (c + 1) * P)
                 nc.tensor.transpose(back[:, cols], turned[:, k, cols], ident[:])
-            nc.scalar.activation(descent[:, k, :], banks[k][:], ACT.Copy, scale=-LR)
+            nc.scalar.activation(descent[:, k, :], dw[k][:], ACT.Copy, scale=-LR)
             nc.scalar.copy(inverse[:, k, :], back[:])
-            win = step_win[k % WINDOWS]
-            nc.vector.tensor_tensor(win[:].indirect(offsets[:]), descent[:, k, :], inverse[:, k, :], ALU.mult)
-            nc.sync.dma_start(out_0[k * P : (k + 1) * P, :], win[:])
+            window = step_windows[k % WINDOWS]
+            nc.vector.tensor_tensor(window[:].indirect(offsets[:]), descent[:, k, :], inverse[:, k, :], ALU.mult)
+            nc.sync.dma_start(out_0[k * P : (k + 1) * P, :], window[:])

from contextlib import ExitStack
import math

import concourse.mybir as mybir
from concourse.masks import make_identity

N, T, D, R = 512, 2048, 512, 1024
LR, RHO, EPS = 0.1, 0.9, 0.001
FLOPS = 4 * R * N * D

F32 = mybir.dt.float32
BF16 = mybir.dt.bfloat16
U32 = mybir.dt.uint32
U16 = mybir.dt.uint16
U8 = mybir.dt.uint8
E4M3 = mybir.dt.float8_e4m3fn_x4
E5M2 = mybir.dt.float8_e5m2_x4
ALU = mybir.AluOpType
ACT = mybir.ActivationFunctionType

P = 128
PACK = 4
KP = P * PACK
PASSES = R // KP
D_TILES = D // P
RUN = 4
STEPS = 128
X_ON_VECTOR = (80, 0)
G_ON_VECTOR = (STEPS, 48)
WINDOWS = 3
EARLY_V = 3


def weave(nc, dst, src, on_vector):
    if on_vector > 0:
        nc.vector.tensor_copy(dst[:, :on_vector], src[:, :on_vector])
    if on_vector < STEPS:
        nc.scalar.copy(dst[:, on_vector:], src[:, on_vector:])


def quantize(nc, pool, grouped, fmt, name, calls=1):
    codes = pool.tile([P, KP], U32, align_bytes=64, name=name + "_codes")
    scales = pool.tile([P, KP], U8, align_bytes=64, name=name + "_scales")
    width = KP // calls
    for c in range(calls):
        words = slice(c * width, (c + 1) * width)
        values = slice(c * width * PACK, (c + 1) * width * PACK)
        nc.vector.quantize_mx(out=codes[:, words].bitcast(fmt), scales=scales[:, words], in_=grouped[:, values])
    return codes, scales


def tile_attend_gkl_rms_kernel(tc, xT, wT, y, wt, xm, vT, offs, out_0, out_1):
    nc = tc.nc
    with ExitStack() as ctx:
        held = ctx.enter_context(tc.tile_pool(name="held", bufs=1))
        table = ctx.enter_context(tc.tile_pool(name="table", bufs=D_TILES))
        pair = ctx.enter_context(tc.tile_pool(name="pair", bufs=PASSES))
        psum = ctx.enter_context(tc.psum_pool(name="psum", bufs=8))

        offsets = held.tile([P, N // 16], U16, name="offsets")
        row_w = held.tile([P, PASSES, PACK], F32, name="row_w")

        x_view = xT[0].rearrange("(p j) r -> p j r", j=PACK)
        w_view = wT.rearrange("(p j) c -> p j c", j=PACK)
        y_view = y[0].rearrange("(g p t) s -> g p t s", g=PASSES, t=PACK)
        m_view = xm[0].rearrange("(g p t) d -> g p t d", g=PASSES, t=PACK)

        def load(pool, tag, name, shape, src):
            dst = pool.tile(shape, F32, tag=tag, name=name)
            nc.sync.dma_start(dst[:], src)
            return dst

        w_planes = [load(table, "w", "w_plane0", [P, T], w_view[:, 0, :])]
        nc.sync.dma_start(offsets[:], offs)
        w_planes.extend(load(table, "w", "w_plane%d" % j, [P, T], w_view[:, j, :]) for j in range(1, PACK))
        x_raw = [
            load(pair, "x", "x_raw%d" % g, [P, PACK, KP], x_view[:, :, g * KP : (g + 1) * KP]) for g in range(PASSES)
        ]
        nc.sync.dma_start(row_w[:], wt[0].rearrange("(g p t) o -> p g (t o)", g=PASSES, t=PACK))
        targets = [load(pair, "y", "targets%d" % g, [P, PACK, N], y_view[g]) for g in range(PASSES)]
        m_raw = [load(pair, "m", "m_raw%d" % g, [P, PACK, D], m_view[g]) for g in range(PASSES)]

        step_windows = []
        for k in range(WINDOWS):
            window = held.tile([P, T], F32, name="step_window%d" % k)
            nc.vector.memset(window[:], 0.0)
            step_windows.append(window)

        ident = held.tile([P, P], F32, name="ident")
        make_identity(nc, ident[:])

        def quantize_x(g):
            grouped = pair.tile([P, KP * PACK], BF16, tag="xg", align_bytes=64, name="x_grouped%d" % g)
            weave(
                nc,
                grouped[:].rearrange("p (t m j) -> p m j t", t=PACK, j=PACK),
                x_raw[g][:].rearrange("p j (m t) -> p m j t", t=PACK),
                X_ON_VECTOR[g],
            )
            return quantize(nc, held, grouped, E4M3, "x%d" % g, PACK)

        def quantize_rows(planes, tag, name, fmt, on_vector):
            grouped = pair.tile([P, KP * PACK], BF16, tag=tag, align_bytes=64, name=name + "_grouped")
            weave(
                nc,
                grouped[:].rearrange("p (c i t) -> p c t i", i=RUN, t=PACK),
                planes[:].rearrange("p t (c i) -> p c t i", i=RUN),
                on_vector,
            )
            return quantize(nc, held, grouped, fmt, name)

        w_grouped = held.tile([P, N * PACK], BF16, align_bytes=64, name="w_grouped")
        w_slots = w_grouped[:].rearrange("p (s j) -> p s j", j=PACK)
        for j in range(PACK):
            nc.vector.tensor_copy(w_slots[:, :, j], w_planes[j][:].indirect(offsets[:]))
        w_codes, w_scales = quantize(nc, held, w_grouped, E4M3, "w")
        x_quantised = [quantize_x(0)]

        def load_v(tag, k):
            return load(table, tag, "v_%s%d" % (tag, k), [P, T], vT[k * P : (k + 1) * P, :])

        v_src = [load_v("v", k) for k in range(EARLY_V)]
        v_dst = [load_v("w", 0)]
        v_src.extend(load_v("v", k) for k in range(EARLY_V, D_TILES))
        v_dst.extend(load_v("w", k) for k in range(1, D_TILES))

        x_quantised.append(quantize_x(1))

        def softmax_parts(g):
            x_codes, x_scales = x_quantised[g]
            neg_max = pair.tile([P, PACK], F32, tag="neg_max", name="neg_max%d" % g)
            total = pair.tile([P, PACK], F32, tag="total", name="total%d" % g)
            exps = pair.tile([P, PACK, N], F32, tag="e", name="exps%d" % g)
            for t in range(PACK):
                cols = slice(t * P, (t + 1) * P)
                scores = psum.tile([P, N], F32, tag="bank", name="scores%d_%d" % (g, t))
                nc.tensor.matmul_mx(
                    out=scores[:], lhsT=x_codes[:, cols].bitcast(E4M3), lhsT_scale=x_scales[:, cols],
                    rhs=w_codes[:].bitcast(E4M3), rhs_scale=w_scales[:], start=True, stop=True,
                )
                nc.vector.tensor_reduce(neg_max[:, t : t + 1], scores[:], mybir.AxisListType.X, ALU.max, negate=True)
                nc.scalar.activation(
                    exps[:, t, :], scores[:], ACT.Exp, bias=neg_max[:, t : t + 1], accum_out=total[:, t : t + 1]
                )
            for t in range(PACK):
                rows = targets[g][:, t, :]
                if g == 0:
                    nc.gpsimd.tensor_scalar(rows, rows, row_w[:, g, t : t + 1], 0.0, ALU.mult, ALU.add)
                else:
                    nc.scalar.activation(rows, rows, ACT.Copy, scale=row_w[:, g, t : t + 1])
            return exps, total

        def gradient(g, exps, total):
            inv = pair.tile([P, PACK], F32, tag="inv", name="inv%d" % g)
            factor = pair.tile([P, PACK], F32, tag="factor", name="factor%d" % g)
            planes = pair.tile([P, PACK, N], BF16, tag="planes", name="planes%d" % g)
            nc.vector.reciprocal(inv[:], total[:])
            nc.vector.tensor_tensor(factor[:], inv[:], row_w[:, g, :], ALU.mult)
            for t in range(PACK):
                nc.vector.scalar_tensor_tensor(
                    planes[:, t, :], exps[:, t, :], factor[:, t : t + 1], targets[g][:, t, :], ALU.mult, ALU.subtract
                )
            return quantize_rows(planes, "gg", "g%d" % g, E5M2, G_ON_VECTOR[g])

        parts = [softmax_parts(g) for g in range(PASSES)]
        g_quantised = []
        m_quantised = []
        for g in range(PASSES):
            m_quantised.append(quantize_rows(m_raw[g], "mg", "m%d" % g, E4M3, 0))
            g_quantised.append(gradient(g, *parts[g]))

        kept = held.tile([P, D_TILES, N], F32, name="kept")
        squares = pair.tile([P, D_TILES, N], F32, tag="x", name="squares")
        descent = pair.tile([P, D_TILES, N], F32, tag="x", name="descent")
        turned = pair.tile([P, D_TILES, N], F32, tag="y", name="turned")
        inverse = pair.tile([P, D_TILES, N], F32, tag="y", name="inverse")

        dw = [psum.tile([P, N], F32, tag="bank", name="dw%d" % k) for k in range(D_TILES)]
        for g in range(PASSES):
            m_codes, m_scales = m_quantised[g]
            g_codes, g_scales = g_quantised[g]
            for k in range(D_TILES):
                cols = slice(k * P, (k + 1) * P)
                nc.tensor.matmul_mx(
                    out=dw[k][:], lhsT=m_codes[:, cols].bitcast(E4M3), lhsT_scale=m_scales[:, cols],
                    rhs=g_codes[:].bitcast(E5M2), rhs_scale=g_scales[:], start=(g == 0), stop=(g == PASSES - 1),
                )

        for k in range(D_TILES):
            nc.scalar.activation(squares[:, k, :], dw[k][:], ACT.Square, scale=math.sqrt(1.0 - RHO))
            nc.vector.tensor_scalar(kept[:, k, :], v_src[k][:].indirect(offsets[:]), RHO, 0.0, ALU.mult, ALU.add)
            nc.vector.tensor_tensor(v_dst[k][:].indirect(offsets[:]), kept[:, k, :], squares[:, k, :], ALU.add)
            nc.sync.dma_start(out_1[k * P : (k + 1) * P, :], v_dst[k][:])

        for k in range(D_TILES):
            grown = psum.tile([P, N], F32, tag="bank", name="grown%d" % k)
            for c in range(N // P):
                cols = slice(c * P, (c + 1) * P)
                nc.tensor.matmul(grown[:, cols], kept[:, k, cols], ident[:], start=True, stop=False, is_transpose=True)
                nc.tensor.matmul(grown[:, cols], squares[:, k, cols], ident[:], start=False, stop=True, is_transpose=True)
            nc.scalar.activation(turned[:, k, :], grown[:], ACT.Sqrt)

        nc.scalar.activation(turned[:], turned[:], ACT.Square, bias=EPS)

        for k in range(D_TILES):
            nc.scalar.activation(turned[:, k, :], turned[:, k, :], ACT.Abs_reciprocal_sqrt)
            back = psum.tile([P, N], F32, tag="bank", name="back%d" % k)
            for c in range(N // P):
                cols = slice(c * P, (c + 1) * P)
                nc.tensor.transpose(back[:, cols], turned[:, k, cols], ident[:])
            nc.scalar.activation(descent[:, k, :], dw[k][:], ACT.Copy, scale=-LR)
            nc.scalar.copy(inverse[:, k, :], back[:])
            window = step_windows[k % WINDOWS]
            nc.vector.tensor_tensor(window[:].indirect(offsets[:]), descent[:, k, :], inverse[:, k, :], ALU.mult)
            nc.sync.dma_start(out_0[k * P : (k + 1) * P, :], window[:])
